import numpy as np, ml_dtypes
CORES = [32,40,48,56,64,72,80,88,96,104,112,120]
N = 12
WB, KB, QP = 2, 1, 128
def setup_inputs(rng):
    return {"q": rng.standard_normal((N, 128, QP), dtype=np.float32).astype(ml_dtypes.bfloat16), "k": rng.standard_normal((N, 128, KB * 128), dtype=np.float32).astype(ml_dtypes.bfloat16), "v": rng.standard_normal((N, 128, KB * 128), dtype=np.float32).astype(ml_dtypes.bfloat16)}
def setup_inputs_big(rng):
    d = setup_inputs(rng)
    for k in ("q", "k", "v"): d[k] = (d[k].astype(np.float32) * 1024.0).astype(d[k].dtype)
    return d
def setup_inputs_small(rng):
    d = setup_inputs(rng)
    for k in ("q", "k", "v"): d[k] = (d[k].astype(np.float32) * (1 / 1024.0)).astype(d[k].dtype)
    return d
def setup_inputs_apart(rng):
    d = setup_inputs(rng)
    f = (10.0 ** rng.permutation(np.linspace(-1.5, 1.5, N))).astype(np.float32).reshape(N, 1, 1)
    for k in ("q", "k", "v"): d[k] = (d[k].astype(np.float32) * f).astype(d[k].dtype)
    return d
def reference(q, k, v):
    Q, K, V = q.astype(np.float64), k.astype(np.float64), v.astype(np.float64)
    y = np.zeros((N, 128, QP))
    for r in range(N):
        for j in range(max(0, r - WB), r + 1):
            for b in range(KB):
                S = np.maximum(K[j][:, 128 * b:128 * b + 128].T @ Q[r], 0.0)
                y[r] += V[j][:, 128 * b:128 * b + 128].T @ S
    return {"y": y.astype(ml_dtypes.bfloat16 if q.dtype != np.float64 else np.float64)}

from concourse.bass import DstId, RemoteDMATransfer
from concourse.mybir import AluOpType

P = 128
BANK = 512

SCRATCH = {
    "stage": ("dram", [2, P, P], "bfloat16"),
    "hop": ("dram", [P, P], "bfloat16"),
    "kv0": ("sbuf", [P, 2 * P], "bfloat16"),
    "kv2": ("sbuf", [P, 2 * P], "bfloat16"),
    "k1": ("sbuf", [P, P], "bfloat16"),
    "v1": ("sbuf", [P, P], "bfloat16"),
    "qs": ("sbuf", [P, P], "bfloat16"),
    "zero": ("sbuf", [P, P], "float32"),
    "s0": ("sbuf", [P, P], "bfloat16"),
    "s1": ("sbuf", [P, P], "bfloat16"),
    "s2": ("sbuf", [P, P], "bfloat16"),
    "yb": ("sbuf", [P, P], "bfloat16"),
    "ps0": ("psum", [P, BANK], "float32"),
    "ps1": ("psum", [P, BANK], "float32"),
    "ps2": ("psum", [P, BANK], "float32"),
    "po": ("psum", [P, BANK], "float32"),
}
SEMAPHORES = ["staged", "own", "ldq", "sent", "hopin", "in1k", "in1v", "in2", "zs",
              "ms0", "ms1", "ms2", "rs0", "rs1", "rs2", "mo", "cp", "st"]


def _bits(mask):
    return [b for b in range(mask.bit_length()) if (mask >> b) & 1]


def _mask(bits):
    m = 0
    for b in bits:
        m |= 1 << b
    return m


def _relay_plan(j, T, topo):
    src, dst = T.cores[j], T.cores[j + 1]
    cand = [c for c in range(topo.CORES_PER_CHIP * topo.CHIPS)
            if topo.chip(c) == topo.chip(src) and T.rank_of(c) is None and topo.may_write(c, dst)]
    near = [c for c in cand if topo.die(c) == topo.die(src)][0]
    far = [c for c in cand if topo.die(c) != topo.die(src)][0]
    eng = _bits(topo.mask(src, near) & topo.mask(src, far))
    half = len(eng) // 2
    return ((near, eng[0:half:2]), (far, eng[half::2]))


def _relay_program(g, core, T, topo, j, which, n_in):
    sem = T.sem
    dst = T.cores[j + 1]
    rid, pid, _se = topo.addr(dst)
    m = topo.mask(core, dst)
    g.wait_ge(sem.hopin, n_in)
    if which == 0:
        g.remote_dma(T.k1[:], T.hop[:], sem.in1k, sem.sent, pid, rid, m)
    else:
        g.remote_dma(T.v1[:], T.hop[:], sem.in1v, sem.sent, pid, rid, m)
    g.wait_ge(sem.sent, len(_bits(m)))


def rank_program(g, core, T, topo):
    n = len(T.cores)
    r = T.rank_of(core)
    if r is None:
        for j in range(n - 1):
            plan = _relay_plan(j, T, topo)
            for which in range(2):
                if plan[which][0] == core:
                    _relay_program(g, core, T, topo, j, which, len(plan[which][1]))
        return

    sem = T.sem
    te, ve = g.tensor, g.vector
    has1, has2 = r + 1 < n, r + 2 < n

    if has1:
        g.sync.dma_start(T.stage[0], T.k[:]).then_inc(sem.staged, 16)
        g.scalar.dma_start(T.stage[1], T.v[:]).then_inc(sem.staged, 16)
    g.sync.dma_start(T.kv0[:, 0:P], T.k[:]).then_inc(sem.own, 16)
    g.scalar.dma_start(T.kv0[:, P:2 * P], T.v[:]).then_inc(sem.own, 16)
    g.sync.dma_start(T.qs[:], T.q[:]).then_inc(sem.ldq, 16)

    sent = 0
    if has1:
        plan = _relay_plan(r, T, topo)
        trs = []
        for which in range(2):
            h, eng = plan[which]
            rid, pid, _se = topo.addr(h)
            trs.append(RemoteDMATransfer(dst_ids=[DstId(rid=rid, pnc=pid)], dma_engine_mask=_mask(eng),
                                         remote_sem=sem.hopin, src=T.stage[which], dst=T.hop[:]))
            sent += len(eng)
        g.wait_ge(sem.staged, 32)
        g.remote_dma_fused(trs, local_sem=sem.sent)
    if has2:
        dst = T.cores[r + 2]
        rid, pid, _se = topo.addr(dst)
        m = topo.mask(core, dst)
        g.wait_ge(sem.own, 32)
        g.remote_dma(T.kv2[:], T.kv0[:], sem.in2, sem.sent, pid, rid, m)
        sent += len(_bits(m))

    blocks = [(T.kv0[:, 0:P], T.kv0[:, P:2 * P], (sem.own, 32), None, T.ps0, T.s0, sem.ms0, sem.rs0)]
    if r >= 2:
        n2 = len(_bits(topo.mask(T.cores[r - 2], core)))
        blocks.append((T.kv2[:, 0:P], T.kv2[:, P:2 * P], (sem.in2, n2), None, T.ps2, T.s2, sem.ms2, sem.rs2))
    if r >= 1:
        nk, nv = [len(_bits(topo.mask(h, core))) for h, _e in _relay_plan(r - 1, T, topo)]
        blocks.append((T.k1[:], T.v1[:], (sem.in1k, nk), (sem.in1v, nv), T.ps1, T.s1, sem.ms1, sem.rs1))

    ve.memset(T.zero[:], 0.0).then_inc(sem.zs, 1)
    ve.wait_ge(sem.zs, 1)
    te.wait_ge(sem.ldq, 16)
    for i, (kb, vb, wk, wv, ps, sb, ms, rs) in enumerate(blocks):
        te.wait_ge(wk[0], wk[1])
        te.matmul(ps[:, 0:P], kb, T.qs[:], start=True, stop=True).then_inc(ms, 1)
        ve.wait_ge(ms, 1)
        ve.tensor_tensor(sb[:], ps[:, 0:P], T.zero[:], op=AluOpType.max).then_inc(rs, 1)
        te.wait_ge(rs, 1)
        if wv is not None:
            te.wait_ge(wv[0], wv[1])
        last = i == len(blocks) - 1
        mm = te.matmul(T.po[:, 0:P], vb, sb[:], start=(i == 0), stop=last)
        if last:
            mm.then_inc(sem.mo, 1)

    ve.wait_ge(sem.mo, 1)
    ve.tensor_copy(T.yb[:], T.po[:, 0:P]).then_inc(sem.cp, 1)
    g.sync.wait_ge(sem.cp, 1)
    g.sync.dma_start(T.y[:], T.yb[:]).then_inc(sem.st, 16)
    g.sync.wait_ge(sem.st, 16)
    if sent:
        g.wait_ge(sem.sent, sent)
